import numpy as np
import ml_dtypes


def mxq(x, axis, fmt="e4m3"):
    dtype, down = {"e4m3": (ml_dtypes.float8_e4m3fn, 7), "e5m2": (ml_dtypes.float8_e5m2, 14)}[fmt]
    v = np.moveaxis(np.asarray(x, np.float32).astype(ml_dtypes.bfloat16).astype(np.float64), axis, -1)
    blocks = v.reshape(v.shape[:-1] + (-1, 32))
    amax = np.abs(blocks).max(-1, keepdims=True)
    byte = np.maximum(np.where(amax > 0, np.frexp(amax)[1] - 1 + 127, 0) - down, 1)
    scale = np.exp2(byte - 127.0)
    codes = (blocks / scale).astype(np.float32).astype(dtype).astype(np.float64)
    return np.moveaxis((codes * scale).reshape(v.shape), -1, axis)


WIDE = False


def mx_kscale(k):
    if not WIDE:
        return np.ones(k)
    levels = np.array([10, -10, 5, -5, 0])
    if k % 512:
        return np.exp2(np.random.permutation(np.resize(levels, k // 32))).repeat(32)
    a = np.empty((k // 512, 16))
    for p in range(k // 512):
        a[p, :8] = np.random.permutation(np.resize(levels, 8))
        for g in range(8):
            far = levels[np.abs(levels - a[p, g]) >= 10]
            a[p, g + 8] = far[np.random.randint(len(far))]
    return np.exp2(a.ravel()).repeat(32)


def f64(x):
    return np.asarray(x).astype(np.float64)


def striped(idx):
    return np.tile(idx.reshape(-1, 16).T, (8, 1)).astype(np.uint16)


def unstriped(offs):
    return offs[:16].T.reshape(-1).astype(np.int64)


def pack_weight(w):
    k, n = w.shape
    w = f64(np.asarray(w, np.float32).astype(ml_dtypes.bfloat16)).reshape(k // 32, 32, n)
    amax = np.abs(w).max(1)
    byte = np.clip(np.where(amax > 0, np.frexp(amax)[1] - 1 + 127 - 7, 1), 1, 254)
    scaled = (w * np.exp2(127.0 - byte)[:, None, :]).reshape(k, n).astype(np.float32)
    words = np.ascontiguousarray(scaled.reshape(k // 512, 128, 4, n).transpose(0, 1, 3, 2)).astype(ml_dtypes.float8_e4m3fn).view(np.uint8)
    return words, np.ascontiguousarray(byte.astype(np.uint8).reshape(k // 512, 16, n))


def unpack_weight(words, scales):
    g, p, n, _ = words.shape
    vals = np.ascontiguousarray(words).view(ml_dtypes.float8_e4m3fn).astype(np.float64) * np.repeat(np.exp2(scales.astype(np.float64) - 127.0), 8, axis=1)[..., None]
    return vals.transpose(0, 1, 3, 2).reshape(g * 512, n)


def relu(v):
    return np.maximum(v, 0.0)


K, T, E, C, N = 512, 1024, 8, 256, 128


def by_expert(wq, xq):
    return np.concatenate([wq[e].T @ xq[:, e * C:(e + 1) * C] for e in range(E)], axis=1)


def setup_inputs():
    n = np.random.standard_normal
    s = mx_kscale(K)[:, None]
    first = np.random.permutation(np.repeat(np.arange(E), T // E))
    second = (first + 1 + np.random.permutation(np.repeat(np.arange(E - 1), -(-T // (E - 1)))[:T])) % E
    while np.bincount(second, minlength=E).max() != T // E:
        load = np.bincount(second, minlength=E); hi, lo = int(load.argmax()), int(load.argmin())
        t = np.flatnonzero((second == hi) & (first != lo))[0]; second[t] = lo
    slot_token = np.empty(E * C, np.int64); pos = np.empty((2, T), np.int64); fill = np.zeros(E, np.int64)
    place = np.stack([np.random.permutation(C) for _ in range(E)])
    for r, deal in enumerate((first, second)):
        for t in np.random.permutation(T):
            e = deal[t]; j = e * C + place[e, fill[e]]; fill[e] += 1; slot_token[j] = t; pos[r, t] = j
    g = np.random.uniform(0.2, 0.8, T)
    packed = [pack_weight(m) for m in n((E, K, N)) / np.sqrt(K) / s[None]]
    return {
        "xT": (n((K, T)) * s).astype(np.float32),
        "w_words": np.stack([m[0] for m in packed]),
        "w_scales": np.stack([m[1] for m in packed]),
        "b": (0.3 * n((N, E))).astype(np.float32),
        "gate": np.stack([np.tile(g, (N, 1)), np.tile(1.0 - g, (N, 1))]).astype(np.float32),
        "offs": striped(slot_token),
        "pos1": striped(pos[0]),
        "pos2": striped(pos[1]),
    }


def reference(xT, w_words, w_scales, b, gate, offs, pos1, pos2):
    idx = unstriped(offs)
    xq = mxq(f64(xT)[:, idx], 0, "e4m3")
    w = np.stack([unpack_weight(w_words[e], w_scales[e]) for e in range(E)])
    y = by_expert(w, xq)
    y = relu(y + np.repeat(f64(b), C, axis=1))
    return f64(gate[0]) * y[:, unstriped(pos1)] + f64(gate[1]) * y[:, unstriped(pos2)]

@@ -1,0 +1,109 @@
+from contextlib import ExitStack
+
+import concourse.mybir as mybir
+
+K, T, E, C, N = 512, 1024, 8, 256, 128
+SLOTS = E * C
+P = 128
+PACK = 4
+
+F32 = mybir.dt.float32
+BF16 = mybir.dt.bfloat16
+U32 = mybir.dt.uint32
+I32 = mybir.dt.int32
+U16 = mybir.dt.uint16
+U8 = mybir.dt.uint8
+FP8X4 = mybir.dt.float8_e4m3fn_x4
+RELU = mybir.ActivationFunctionType.Relu
+ADD = mybir.AluOpType.add
+MAX = mybir.AluOpType.max
+MULT = mybir.AluOpType.mult
+
+FLOPS = 2 * K * N * SLOTS
+
+CHUNKS = ((0, 256, 128), (256, 256, 128), (512, 256, 128), (768, 256, 160))
+PIECES = ((0, 768), (768, 768), (1536, 256), (1792, 256))
+TOKEN_PIECES = ((0, 512), (512, 256), (768, 256))
+
+
+def tile_routed_moe_kernel(tc, xT, w_words, w_scales, b, gate, offs, pos1, pos2, out):
+    nc = tc.nc
+    with ExitStack() as ctx:
+        keep = ctx.enter_context(tc.tile_pool(name="keep", bufs=1))
+        stage = ctx.enter_context(tc.tile_pool(name="stage", bufs=4))
+        psum = ctx.enter_context(tc.psum_pool(name="psum", bufs=8))
+
+        offs_sb = keep.tile([P, SLOTS // 16], U16, name="offs_sb")
+        pos1_sb = keep.tile([P, T // 16], U16, name="pos1_sb")
+        pos2_sb = keep.tile([P, T // 16], U16, name="pos2_sb")
+        x_words = keep.tile([P, T], U32, name="x_words", align_bytes=64)
+        x_scales = keep.tile([P, T], U8, name="x_scales", align_bytes=64)
+        s_words = keep.tile([P, SLOTS], U32, name="s_words", align_bytes=64)
+        s_scales = keep.tile([P, SLOTS], U8, name="s_scales", align_bytes=64)
+        w_sb = keep.tile([P, E, N * PACK], U8, name="w_sb", align_bytes=64)
+        ws_sb = keep.tile([P, E, N], U8, name="ws_sb", align_bytes=64)
+        b_sb = keep.tile([P, E], F32, name="b_sb")
+        gate1_sb = keep.tile([P, T], F32, name="gate1_sb")
+        gate2_sb = keep.tile([P, T], F32, name="gate2_sb")
+        y = keep.tile([P, SLOTS], F32, name="y")
+
+        nc.gpsimd.memset(x_scales[:], 0)
+        nc.vector.memset(ws_sb[:].rearrange("p e n -> p (e n)").bitcast(I32), 0)
+
+        x_rows = xT.rearrange("(p j) t -> p j t", j=PACK)
+        raws = []
+        for t0, n, nv in CHUNKS:
+            raw = stage.tile([P, PACK, n], F32, name="raw")
+            nc.sync.dma_start(out=raw[:], in_=x_rows[:, :, t0 : t0 + n])
+            raws.append(raw)
+        nc.sync.dma_start(offs_sb[:], offs)
+        for q in range(4):
+            nc.sync.dma_start(
+                out=ws_sb[32 * q : 32 * q + 4, :, :].bitcast(I32),
+                in_=w_scales[:, 0, 4 * q : 4 * q + 4, :].rearrange("e q n -> q e n").bitcast(I32),
+            )
+        nc.sync.dma_start(out=w_sb[:], in_=w_words.rearrange("e a p n r -> p (e a) (n r)"))
+        nc.sync.dma_start(out=b_sb[:], in_=b)
+        nc.sync.dma_start(pos1_sb[:], pos1)
+        nc.sync.dma_start(out=gate1_sb[:], in_=gate[0])
+        nc.sync.dma_start(pos2_sb[:], pos2)
+        nc.sync.dma_start(out=gate2_sb[:], in_=gate[1])
+
+        for (t0, n, nv), raw in zip(CHUNKS, raws):
+            grouped = stage.tile([P, n, PACK], BF16, name="grouped", align_bytes=64)
+            nc.vector.tensor_copy(out=grouped[:, 0:nv, :], in_=raw[:, :, 0:nv].rearrange("p j n -> p n j"))
+            nc.scalar.copy(out=grouped[:, nv:n, :], in_=raw[:, :, nv:n].rearrange("p j n -> p n j"))
+            nc.vector.quantize_mx(
+                out=x_words[:, t0 : t0 + n].bitcast(FP8X4),
+                scales=x_scales[:, t0 : t0 + n],
+                in_=grouped[:].rearrange("p n j -> p (n j)"),
+            )
+
+        for j0, n in PIECES:
+            cols = offs_sb[:, j0 // 16 : (j0 + n) // 16]
+            nc.vector.tensor_copy(out=s_scales[:, j0 : j0 + n], in_=x_scales[:].indirect(cols))
+            nc.vector.tensor_copy(out=s_words[:, j0 : j0 + n], in_=x_words[:].indirect(cols))
+            for e in range(j0 // C, (j0 + n) // C):
+                slots = slice(e * C, (e + 1) * C)
+                acc = psum.tile([N, C], F32, name="acc")
+                nc.tensor.matmul_mx(
+                    out=acc[:],
+                    lhsT=w_sb[:, e, :].bitcast(FP8X4),
+                    lhsT_scale=ws_sb[:, e, :],
+                    rhs=s_words[:, slots].bitcast(FP8X4),
+                    rhs_scale=s_scales[:, slots],
+                    start=True,
+                    stop=True,
+                )
+                nc.scalar.activation(y[:, slots], acc[:], RELU, bias=b_sb[:, e : e + 1])
+
+        for t0, n in TOKEN_PIECES:
+            tokens = slice(t0, t0 + n)
+            cols = slice(t0 // 16, (t0 + n) // 16)
+            part1 = stage.tile([P, n], F32, name="part1")
+            part2 = stage.tile([P, n], F32, name="part2")
+            total = stage.tile([P, n], F32, name="total")
+            nc.vector.tensor_tensor(part1[:], y[:].indirect(pos1_sb[:, cols]), gate1_sb[:, tokens], MULT)
+            nc.vector.tensor_tensor(part2[:], y[:].indirect(pos2_sb[:, cols]), gate2_sb[:, tokens], MULT)
+            nc.vector.tensor_tensor(total[:], part1[:], part2[:], ADD)
+            nc.sync.dma_start(out=out[:, tokens], in_=total[:])

@@ -21,9 +21,11 @@ MULT = mybir.AluOpType.mult
 
 FLOPS = 2 * K * N * SLOTS
 
-CHUNKS = ((0, 256, 128), (256, 256, 128), (512, 256, 128), (768, 256, 160))
-PIECES = ((0, 768), (768, 768), (1536, 256), (1792, 256))
-TOKEN_PIECES = ((0, 512), (512, 256), (768, 256))
+LOADS = ((0, 512), (512, 256), (768, 256))
+CHUNKS = ((0, 0, 512, 256), (1, 512, 256, 128), (2, 768, 128, 80), (2, 896, 128, 80))
+BYTE_PIECES = ((0, 768), (768, 768), (1536, 512))
+WORD_PIECES = (((0, 768),), ((768, 768),), ((1536, 256), (1792, 256)))
+TOKEN_PIECES = ((0, 512), (512, 384), (896, 128))
 
 
 def tile_routed_moe_kernel(tc, xT, w_words, w_scales, b, gate, offs, pos1, pos2, out):
@@ -52,11 +54,12 @@ def tile_routed_moe_kernel(tc, xT, w_words, w_scales, b, gate, offs, pos1, pos2,
 
         x_rows = xT.rearrange("(p j) t -> p j t", j=PACK)
         raws = []
-        for t0, n, nv in CHUNKS:
+        for t0, n in LOADS:
             raw = stage.tile([P, PACK, n], F32, name="raw")
             nc.sync.dma_start(out=raw[:], in_=x_rows[:, :, t0 : t0 + n])
             raws.append(raw)
-        nc.sync.dma_start(offs_sb[:], offs)
+            if t0 == 0:
+                nc.sync.dma_start(offs_sb[:], offs)
         for q in range(4):
             nc.sync.dma_start(
                 out=ws_sb[32 * q : 32 * q + 4, :, :].bitcast(I32),
@@ -69,41 +72,60 @@ def tile_routed_moe_kernel(tc, xT, w_words, w_scales, b, gate, offs, pos1, pos2,
         nc.sync.dma_start(pos2_sb[:], pos2)
         nc.sync.dma_start(out=gate2_sb[:], in_=gate[1])
 
-        for (t0, n, nv), raw in zip(CHUNKS, raws):
+        def interleave(chunk):
+            load, t0, n, nv = chunk
+            raw, r0 = raws[load], t0 - LOADS[load][0]
             grouped = stage.tile([P, n, PACK], BF16, name="grouped", align_bytes=64)
-            nc.vector.tensor_copy(out=grouped[:, 0:nv, :], in_=raw[:, :, 0:nv].rearrange("p j n -> p n j"))
-            nc.scalar.copy(out=grouped[:, nv:n, :], in_=raw[:, :, nv:n].rearrange("p j n -> p n j"))
+            nc.vector.tensor_copy(out=grouped[:, 0:nv, :], in_=raw[:, :, r0 : r0 + nv].rearrange("p j n -> p n j"))
+            nc.scalar.copy(out=grouped[:, nv:n, :], in_=raw[:, :, r0 + nv : r0 + n].rearrange("p j n -> p n j"))
+            return grouped
+
+        def quantise(chunk, grouped):
+            load, t0, n, nv = chunk
             nc.vector.quantize_mx(
                 out=x_words[:, t0 : t0 + n].bitcast(FP8X4),
                 scales=x_scales[:, t0 : t0 + n],
                 in_=grouped[:].rearrange("p n j -> p (n j)"),
             )
 
-        for j0, n in PIECES:
-            cols = offs_sb[:, j0 // 16 : (j0 + n) // 16]
-            nc.vector.tensor_copy(out=s_scales[:, j0 : j0 + n], in_=x_scales[:].indirect(cols))
-            nc.vector.tensor_copy(out=s_words[:, j0 : j0 + n], in_=x_words[:].indirect(cols))
-            for e in range(j0 // C, (j0 + n) // C):
-                slots = slice(e * C, (e + 1) * C)
-                acc = psum.tile([N, C], F32, name="acc")
-                nc.tensor.matmul_mx(
-                    out=acc[:],
-                    lhsT=w_sb[:, e, :].bitcast(FP8X4),
-                    lhsT_scale=ws_sb[:, e, :],
-                    rhs=s_words[:, slots].bitcast(FP8X4),
-                    rhs_scale=s_scales[:, slots],
-                    start=True,
-                    stop=True,
-                )
-                nc.scalar.activation(y[:, slots], acc[:], RELU, bias=b_sb[:, e : e + 1])
+        for load in range(len(LOADS)):
+            chunks = [c for c in CHUNKS if c[0] == load]
+            grouped = [interleave(c) for c in chunks]
+            for c, g in zip(chunks, grouped):
+                quantise(c, g)
 
+        for (b0, bn), words in zip(BYTE_PIECES, WORD_PIECES):
+            nc.vector.tensor_copy(
+                out=s_scales[:, b0 : b0 + bn], in_=x_scales[:].indirect(offs_sb[:, b0 // 16 : (b0 + bn) // 16])
+            )
+            for j0, n in words:
+                nc.vector.tensor_copy(
+                    out=s_words[:, j0 : j0 + n], in_=x_words[:].indirect(offs_sb[:, j0 // 16 : (j0 + n) // 16])
+                )
+                for e in range(j0 // C, (j0 + n) // C):
+                    slots = slice(e * C, (e + 1) * C)
+                    acc = psum.tile([N, C], F32, name="acc")
+                    nc.tensor.matmul_mx(
+                        out=acc[:],
+                        lhsT=w_sb[:, e, :].bitcast(FP8X4),
+                        lhsT_scale=ws_sb[:, e, :],
+                        rhs=s_words[:, slots].bitcast(FP8X4),
+                        rhs_scale=s_scales[:, slots],
+                        start=True,
+                        stop=True,
+                    )
+                    nc.scalar.activation(y[:, slots], acc[:], RELU, bias=b_sb[:, e : e + 1])
+
+        part1 = keep.tile([P, T], F32, name="part1")
+        nc.vector.tensor_tensor(part1[:], y[:].indirect(pos1_sb[:]), gate1_sb[:], MULT)
+        part2 = []
         for t0, n in TOKEN_PIECES:
-            tokens = slice(t0, t0 + n)
-            cols = slice(t0 // 16, (t0 + n) // 16)
-            part1 = stage.tile([P, n], F32, name="part1")
-            part2 = stage.tile([P, n], F32, name="part2")
+            p2 = stage.tile([P, n], F32, name="p2")
+            nc.vector.tensor_tensor(
+                p2[:], y[:].indirect(pos2_sb[:, t0 // 16 : (t0 + n) // 16]), gate2_sb[:, t0 : t0 + n], MULT
+            )
+            part2.append(p2)
+        for (t0, n), p2 in zip(TOKEN_PIECES, part2):
             total = stage.tile([P, n], F32, name="total")
-            nc.vector.tensor_tensor(part1[:], y[:].indirect(pos1_sb[:, cols]), gate1_sb[:, tokens], MULT)
-            nc.vector.tensor_tensor(part2[:], y[:].indirect(pos2_sb[:, cols]), gate2_sb[:, tokens], MULT)
-            nc.vector.tensor_tensor(total[:], part1[:], part2[:], ADD)
-            nc.sync.dma_start(out=out[:, tokens], in_=total[:])
+            nc.vector.tensor_tensor(total[:], part1[:, t0 : t0 + n], p2[:], ADD)
+            nc.sync.dma_start(out=out[:, t0 : t0 + n], in_=total[:])

@@ -21,11 +21,11 @@ MULT = mybir.AluOpType.mult
 
 FLOPS = 2 * K * N * SLOTS
 
-LOADS = ((0, 512), (512, 256), (768, 256))
-CHUNKS = ((0, 0, 512, 256), (1, 512, 256, 128), (2, 768, 128, 80), (2, 896, 128, 80))
+LOADS = ((0, 384), (384, 384), (768, 256))
+CHUNKS = ((0, 0, 256, 144), (0, 256, 128, 80), (1, 384, 256, 144), (1, 640, 128, 80), (2, 768, 256, 176))
 BYTE_PIECES = ((0, 768), (768, 768), (1536, 512))
 WORD_PIECES = (((0, 768),), ((768, 768),), ((1536, 256), (1792, 256)))
-TOKEN_PIECES = ((0, 512), (512, 384), (896, 128))
+TOKEN_PIECES = ((0, 640), (640, 256), (896, 128))
 
 
 def tile_routed_moe_kernel(tc, xT, w_words, w_scales, b, gate, offs, pos1, pos2, out):
@@ -55,7 +55,7 @@ def tile_routed_moe_kernel(tc, xT, w_words, w_scales, b, gate, offs, pos1, pos2,
         x_rows = xT.rearrange("(p j) t -> p j t", j=PACK)
         raws = []
         for t0, n in LOADS:
-            raw = stage.tile([P, PACK, n], F32, name="raw")
+            raw = stage.tile([P, PACK, n], F32, name="raw", bufs=len(LOADS))
             nc.sync.dma_start(out=raw[:], in_=x_rows[:, :, t0 : t0 + n])
             raws.append(raw)
             if t0 == 0:
@@ -75,7 +75,7 @@ def tile_routed_moe_kernel(tc, xT, w_words, w_scales, b, gate, offs, pos1, pos2,
         def interleave(chunk):
             load, t0, n, nv = chunk
             raw, r0 = raws[load], t0 - LOADS[load][0]
-            grouped = stage.tile([P, n, PACK], BF16, name="grouped", align_bytes=64)
+            grouped = stage.tile([P, n, PACK], BF16, name="grouped", bufs=len(CHUNKS), align_bytes=64)
             nc.vector.tensor_copy(out=grouped[:, 0:nv, :], in_=raw[:, :, r0 : r0 + nv].rearrange("p j n -> p n j"))
             nc.scalar.copy(out=grouped[:, nv:n, :], in_=raw[:, :, r0 + nv : r0 + n].rearrange("p j n -> p n j"))
             return grouped
@@ -118,14 +118,23 @@ def tile_routed_moe_kernel(tc, xT, w_words, w_scales, b, gate, offs, pos1, pos2,
 
         part1 = keep.tile([P, T], F32, name="part1")
         nc.vector.tensor_tensor(part1[:], y[:].indirect(pos1_sb[:]), gate1_sb[:], MULT)
-        part2 = []
-        for t0, n in TOKEN_PIECES:
-            p2 = stage.tile([P, n], F32, name="p2")
+
+        def second_part(t0, n):
+            part2 = stage.tile([P, n], F32, name="part2")
             nc.vector.tensor_tensor(
-                p2[:], y[:].indirect(pos2_sb[:, t0 // 16 : (t0 + n) // 16]), gate2_sb[:, t0 : t0 + n], MULT
+                part2[:], y[:].indirect(pos2_sb[:, t0 // 16 : (t0 + n) // 16]), gate2_sb[:, t0 : t0 + n], MULT
             )
-            part2.append(p2)
-        for (t0, n), p2 in zip(TOKEN_PIECES, part2):
+            return part2
+
+        def add_and_store(t0, n, part2):
             total = stage.tile([P, n], F32, name="total")
-            nc.vector.tensor_tensor(total[:], part1[:, t0 : t0 + n], p2[:], ADD)
+            nc.vector.tensor_tensor(total[:], part1[:, t0 : t0 + n], part2[:], ADD)
             nc.sync.dma_start(out=out[:, t0 : t0 + n], in_=total[:])
+
+        waiting = None
+        for t0, n in TOKEN_PIECES:
+            part2 = second_part(t0, n)
+            if waiting is not None:
+                add_and_store(*waiting)
+            waiting = (t0, n, part2)
+        add_and_store(*waiting)

@@ -21,8 +21,8 @@ MULT = mybir.AluOpType.mult
 
 FLOPS = 2 * K * N * SLOTS
 
-LOADS = ((0, 384), (384, 384), (768, 256))
-CHUNKS = ((0, 0, 256, 144), (0, 256, 128, 80), (1, 384, 256, 144), (1, 640, 128, 80), (2, 768, 256, 176))
+LOADS = ((0, 256), (256, 256), (512, 384), (896, 128))
+CHUNKS = ((0, 0, 256, 144), (1, 256, 256, 144), (2, 512, 256, 144), (2, 768, 128, 80), (3, 896, 128, 88))
 BYTE_PIECES = ((0, 768), (768, 768), (1536, 512))
 WORD_PIECES = (((0, 768),), ((768, 768),), ((1536, 256), (1792, 256)))
 TOKEN_PIECES = ((0, 640), (640, 256), (896, 128))

from contextlib import ExitStack

import concourse.mybir as mybir

K, T, E, C, N = 512, 1024, 8, 256, 128
SLOTS = E * C
P = 128
PACK = 4

F32 = mybir.dt.float32
BF16 = mybir.dt.bfloat16
U32 = mybir.dt.uint32
I32 = mybir.dt.int32
U16 = mybir.dt.uint16
U8 = mybir.dt.uint8
FP8X4 = mybir.dt.float8_e4m3fn_x4
RELU = mybir.ActivationFunctionType.Relu
ADD = mybir.AluOpType.add
MAX = mybir.AluOpType.max
MULT = mybir.AluOpType.mult

FLOPS = 2 * K * N * SLOTS

LOADS = ((0, 256), (256, 256), (512, 384), (896, 128))
CHUNKS = ((0, 0, 256, 144), (1, 256, 256, 144), (2, 512, 256, 144), (2, 768, 128, 80), (3, 896, 128, 88))
BYTE_PIECES = ((0, 768), (768, 768), (1536, 512))
WORD_PIECES = (((0, 768),), ((768, 768),), ((1536, 256), (1792, 256)))
TOKEN_PIECES = ((0, 640), (640, 256), (896, 128))


def tile_routed_moe_kernel(tc, xT, w_words, w_scales, b, gate, offs, pos1, pos2, out):
    nc = tc.nc
    with ExitStack() as ctx:
        keep = ctx.enter_context(tc.tile_pool(name="keep", bufs=1))
        stage = ctx.enter_context(tc.tile_pool(name="stage", bufs=4))
        psum = ctx.enter_context(tc.psum_pool(name="psum", bufs=8))

        offs_sb = keep.tile([P, SLOTS // 16], U16, name="offs_sb")
        pos1_sb = keep.tile([P, T // 16], U16, name="pos1_sb")
        pos2_sb = keep.tile([P, T // 16], U16, name="pos2_sb")
        x_words = keep.tile([P, T], U32, name="x_words", align_bytes=64)
        x_scales = keep.tile([P, T], U8, name="x_scales", align_bytes=64)
        s_words = keep.tile([P, SLOTS], U32, name="s_words", align_bytes=64)
        s_scales = keep.tile([P, SLOTS], U8, name="s_scales", align_bytes=64)
        w_sb = keep.tile([P, E, N * PACK], U8, name="w_sb", align_bytes=64)
        ws_sb = keep.tile([P, E, N], U8, name="ws_sb", align_bytes=64)
        b_sb = keep.tile([P, E], F32, name="b_sb")
        gate1_sb = keep.tile([P, T], F32, name="gate1_sb")
        gate2_sb = keep.tile([P, T], F32, name="gate2_sb")
        y = keep.tile([P, SLOTS], F32, name="y")

        nc.gpsimd.memset(x_scales[:], 0)
        nc.vector.memset(ws_sb[:].rearrange("p e n -> p (e n)").bitcast(I32), 0)

        x_rows = xT.rearrange("(p j) t -> p j t", j=PACK)
        raws = []
        for t0, n in LOADS:
            raw = stage.tile([P, PACK, n], F32, name="raw", bufs=len(LOADS))
            nc.sync.dma_start(out=raw[:], in_=x_rows[:, :, t0 : t0 + n])
            raws.append(raw)
            if t0 == 0:
                nc.sync.dma_start(offs_sb[:], offs)
        for q in range(4):
            nc.sync.dma_start(
                out=ws_sb[32 * q : 32 * q + 4, :, :].bitcast(I32),
                in_=w_scales[:, 0, 4 * q : 4 * q + 4, :].rearrange("e q n -> q e n").bitcast(I32),
            )
        nc.sync.dma_start(out=w_sb[:], in_=w_words.rearrange("e a p n r -> p (e a) (n r)"))
        nc.sync.dma_start(out=b_sb[:], in_=b)
        nc.sync.dma_start(pos1_sb[:], pos1)
        nc.sync.dma_start(out=gate1_sb[:], in_=gate[0])
        nc.sync.dma_start(pos2_sb[:], pos2)
        nc.sync.dma_start(out=gate2_sb[:], in_=gate[1])

        def interleave(chunk):
            load, t0, n, nv = chunk
            raw, r0 = raws[load], t0 - LOADS[load][0]
            grouped = stage.tile([P, n, PACK], BF16, name="grouped", bufs=len(CHUNKS), align_bytes=64)
            nc.vector.tensor_copy(out=grouped[:, 0:nv, :], in_=raw[:, :, r0 : r0 + nv].rearrange("p j n -> p n j"))
            nc.scalar.copy(out=grouped[:, nv:n, :], in_=raw[:, :, r0 + nv : r0 + n].rearrange("p j n -> p n j"))
            return grouped

        def quantise(chunk, grouped):
            load, t0, n, nv = chunk
            nc.vector.quantize_mx(
                out=x_words[:, t0 : t0 + n].bitcast(FP8X4),
                scales=x_scales[:, t0 : t0 + n],
                in_=grouped[:].rearrange("p n j -> p (n j)"),
            )

        for load in range(len(LOADS)):
            chunks = [c for c in CHUNKS if c[0] == load]
            grouped = [interleave(c) for c in chunks]
            for c, g in zip(chunks, grouped):
                quantise(c, g)

        for (b0, bn), words in zip(BYTE_PIECES, WORD_PIECES):
            nc.vector.tensor_copy(
                out=s_scales[:, b0 : b0 + bn], in_=x_scales[:].indirect(offs_sb[:, b0 // 16 : (b0 + bn) // 16])
            )
            for j0, n in words:
                nc.vector.tensor_copy(
                    out=s_words[:, j0 : j0 + n], in_=x_words[:].indirect(offs_sb[:, j0 // 16 : (j0 + n) // 16])
                )
                for e in range(j0 // C, (j0 + n) // C):
                    slots = slice(e * C, (e + 1) * C)
                    acc = psum.tile([N, C], F32, name="acc")
                    nc.tensor.matmul_mx(
                        out=acc[:],
                        lhsT=w_sb[:, e, :].bitcast(FP8X4),
                        lhsT_scale=ws_sb[:, e, :],
                        rhs=s_words[:, slots].bitcast(FP8X4),
                        rhs_scale=s_scales[:, slots],
                        start=True,
                        stop=True,
                    )
                    nc.scalar.activation(y[:, slots], acc[:], RELU, bias=b_sb[:, e : e + 1])

        part1 = keep.tile([P, T], F32, name="part1")
        nc.vector.tensor_tensor(part1[:], y[:].indirect(pos1_sb[:]), gate1_sb[:], MULT)

        def second_part(t0, n):
            part2 = stage.tile([P, n], F32, name="part2")
            nc.vector.tensor_tensor(
                part2[:], y[:].indirect(pos2_sb[:, t0 // 16 : (t0 + n) // 16]), gate2_sb[:, t0 : t0 + n], MULT
            )
            return part2

        def add_and_store(t0, n, part2):
            total = stage.tile([P, n], F32, name="total")
            nc.vector.tensor_tensor(total[:], part1[:, t0 : t0 + n], part2[:], ADD)
            nc.sync.dma_start(out=out[:, t0 : t0 + n], in_=total[:])

        waiting = None
        for t0, n in TOKEN_PIECES:
            part2 = second_part(t0, n)
            if waiting is not None:
                add_and_store(*waiting)
            waiting = (t0, n, part2)
        add_and_store(*waiting)
